import numpy as np
import ml_dtypes


def mxq(x, axis, fmt="e4m3"):
    dtype, down = {"e4m3": (ml_dtypes.float8_e4m3fn, 7), "e5m2": (ml_dtypes.float8_e5m2, 14)}[fmt]
    v = np.moveaxis(np.asarray(x, np.float32).astype(ml_dtypes.bfloat16).astype(np.float64), axis, -1)
    blocks = v.reshape(v.shape[:-1] + (-1, 32))
    amax = np.abs(blocks).max(-1, keepdims=True)
    byte = np.maximum(np.where(amax > 0, np.frexp(amax)[1] - 1 + 127, 0) - down, 1)
    scale = np.exp2(byte - 127.0)
    codes = (blocks / scale).astype(np.float32).astype(dtype).astype(np.float64)
    return np.moveaxis((codes * scale).reshape(v.shape), -1, axis)


WIDE = False


def mx_kscale(k):
    if not WIDE:
        return np.ones(k)
    levels = np.array([10, -10, 5, -5, 0])
    if k % 512:
        return np.exp2(np.random.permutation(np.resize(levels, k // 32))).repeat(32)
    a = np.empty((k // 512, 16))
    for p in range(k // 512):
        a[p, :8] = np.random.permutation(np.resize(levels, 8))
        for g in range(8):
            far = levels[np.abs(levels - a[p, g]) >= 10]
            a[p, g + 8] = far[np.random.randint(len(far))]
    return np.exp2(a.ravel()).repeat(32)


def f64(x):
    return np.asarray(x).astype(np.float64)


def striped8(idx):
    return np.asarray(idx).reshape(8, -1, 16).transpose(0, 2, 1).reshape(128, -1).astype(np.uint16)


def unstriped8(offs):
    return offs.reshape(8, 16, -1).transpose(0, 2, 1).reshape(8, -1).astype(np.int64)


def pick8(x, idx, run):
    r = np.arange(len(x))
    return x[r[:, None], idx[r % (8 * run) // run]]


E2M1 = np.array([0.0, 0.5, 1.0, 1.5, 2.0, 3.0, 4.0, 6.0, -0.0, -0.5, -1.0, -1.5, -2.0, -3.0, -4.0, -6.0])


def pack_weight(w, fmt):
    k, n = w.shape
    w = f64(np.asarray(w, np.float32).astype(ml_dtypes.bfloat16)).reshape(k // 32, 32, n)
    amax = np.abs(w).max(1)
    if fmt == "e4m3":
        byte = np.frexp(amax)[1] - 1 + 127 - 7
    else:
        mant, ex = np.frexp(amax / 6.0)
        byte = np.where(mant > 0.5, ex, ex - 1) + 127
    byte = np.clip(np.where(amax > 0, byte, 1), 1, 254)
    scaled = (w * np.exp2(127.0 - byte)[:, None, :]).reshape(k, n).astype(np.float32)
    by_word = np.ascontiguousarray(scaled.reshape(k // 512, 128, 4, n).transpose(0, 1, 3, 2))
    if fmt == "e4m3":
        words = by_word.astype(ml_dtypes.float8_e4m3fn).view(np.uint8)
    else:
        c = by_word.astype(ml_dtypes.float4_e2m1fn).view(np.uint8) & 0xF
        words = (c[..., 0::2] | (c[..., 1::2] << 4)).reshape(k // 512, 128, 2 * n)
    return np.ascontiguousarray(words), np.ascontiguousarray(byte.astype(np.uint8).reshape(k // 512, 16, n))


def unpack_weight(words, scales, fmt):
    g, _, n = scales.shape
    words = np.ascontiguousarray(words).reshape(g, 128, n, -1)
    if fmt == "e4m3":
        vals = words.view(ml_dtypes.float8_e4m3fn).astype(np.float64)
    else:
        nib = np.empty((g, 128, n, 4), np.uint8)
        nib[..., 0::2] = words & 0xF
        nib[..., 1::2] = words >> 4
        vals = E2M1[nib]
    vals = vals * np.repeat(np.exp2(scales.astype(np.float64) - 127.0), 8, axis=1)[..., None]
    return vals.transpose(0, 1, 3, 2).reshape(g * 512, n)


def bf(x):
    return np.asarray(x, np.float32).astype(ml_dtypes.bfloat16)


def planes(Y):
    r, m = Y.shape
    b = f64(bf(Y)).reshape(r // 32, 32, m)
    amax = np.abs(b).max(1)
    byte = np.clip(np.where(amax > 0, np.frexp(amax)[1] - 1 + 127 - 7, 1), 1, 254)
    codes = (b * np.exp2(127.0 - byte)[:, None, :]).reshape(r, m).astype(np.float32).astype(ml_dtypes.float8_e4m3fn).view(np.uint8)
    words = codes.reshape(r // 512, 128, 4, m).transpose(0, 1, 3, 2)
    return np.ascontiguousarray(words), np.ascontiguousarray(byte.astype(np.uint8).reshape(r // 512, 16, m))


K, T, J, N = 512, 512, 512, 512


def setup_inputs():
    n = np.random.standard_normal
    idx = np.stack([np.random.randint(0, T, J) for _ in range(8)])
    fk = mx_kscale(K)
    wp = pack_weight(n((K, N)) * 1 / np.sqrt(K) * fk[:, None], "e2m1")
    return {
        "xt": (n((K, T)) / fk[:, None]).astype(np.float32),
        "w_words": wp[0],
        "w_scales": wp[1],
        "st": (np.random.uniform(0.5, 2.0, (N, 1))).astype(np.float32),
        "offs": striped8(idx),
    }


def reference(xt, w_words, w_scales, st, offs):
    idx = unstriped8(offs)
    wu = unpack_weight(w_words, w_scales, "e2m1")
    xtq = mxq(f64(xt), 0, "e4m3")
    z = wu.T @ xtq
    u = pick8(z, idx, 64)
    us_ = np.pad(u, ((0, 0), (1, 0)))[:, :J]
    y = f64(st) * (u - us_) + 0.5 * u
    words, scales = planes(y)
    return y, words, scales

@@ -1,0 +1,122 @@
+from contextlib import ExitStack
+
+import concourse.mybir as mybir
+
+K, T, J, N = 512, 512, 512, 512
+FLOPS = 2 * K * N * T
+
+F32 = mybir.dt.float32
+BF16 = mybir.dt.bfloat16
+I32 = mybir.dt.int32
+U32 = mybir.dt.uint32
+U16 = mybir.dt.uint16
+U8 = mybir.dt.uint8
+FP8X4 = mybir.dt.float8_e4m3fn_x4
+FP4X4 = mybir.dt.float4_e2m1fn_x4
+ALU = mybir.AluOpType
+COPY = mybir.ActivationFunctionType.Copy
+
+P = 128
+PACK = 4
+LEAD = 8
+X_CHUNKS = ((0, 256), (256, 512))
+X_SPLIT = 168
+J_CHUNKS = ((0, 256), (256, 512))
+Y_SPLIT = 168
+
+
+def tile_list_head_steps_in_time_pl_kernel(tc, xt, w_words, w_scales, st, offs, out_0, out_1, out_2):
+    nc = tc.nc
+    with ExitStack() as ctx:
+        held = ctx.enter_context(tc.tile_pool(name="held", bufs=1))
+        picks = ctx.enter_context(tc.tile_pool(name="picks", bufs=5))
+        psum = ctx.enter_context(tc.psum_pool(name="psum", bufs=1))
+
+        x_rows = xt.rearrange("(p i) c -> p i c", i=PACK)
+        x_raw = []
+        for c, (a, b) in enumerate(X_CHUNKS):
+            tile = held.tile([P, PACK, b - a], F32, name="x_raw%d" % c)
+            nc.sync.dma_start(out=tile[:], in_=x_rows[:, :, a:b])
+            x_raw.append(tile)
+        offsets = held.tile([P, J // 16], U16, name="offsets")
+        nc.sync.dma_start(offsets[:], offs)
+
+        w_raw = held.tile([P, 2 * N], U8, name="w_raw")
+        nc.scalar.dma_start(out=w_raw[:].bitcast(I32), in_=w_words[0].bitcast(I32))
+        ws_raw = held.tile([P, N], U8, name="ws_raw")
+        nc.gpsimd.memset(ws_raw[:].bitcast(I32), 0)
+        for q in range(4):
+            nc.scalar.dma_start(out=ws_raw[32 * q : 32 * q + 4, :].bitcast(I32),
+                                in_=w_scales[0, 4 * q : 4 * q + 4, :].bitcast(I32))
+        step = held.tile([P, PACK], F32, name="step")
+        nc.gpsimd.dma_start(out=step[:], in_=st.rearrange("(p i) o -> p (i o)", i=PACK))
+        own = held.tile([P, PACK], F32, name="own")
+        nc.gpsimd.tensor_scalar(own[:], step[:], 1.0, 0.5, ALU.mult, ALU.add)
+
+        w_codes = held.tile([P, 2 * N], U8, name="w_codes", align_bytes=64)
+        nc.vector.tensor_copy(out=w_codes[:].bitcast(U16).rearrange("p (i m) -> p i m", i=PACK),
+                              in_=w_raw[:].bitcast(U16).rearrange("p (m i) -> p i m", i=PACK))
+        w_scale = held.tile([P, N], U8, name="w_scale", align_bytes=64)
+        nc.vector.tensor_copy(out=w_scale[:].rearrange("p (i m) -> p i m", i=PACK),
+                              in_=ws_raw[:].rearrange("p (m i) -> p i m", i=PACK))
+
+        before = [held.tile([P, LEAD + J], F32, name="before%d" % i) for i in range(PACK)]
+        for i in range(PACK):
+            nc.vector.memset(before[i][:, LEAD - 1 : LEAD], 0.0)
+
+        z = [held.tile([P, T], F32, name="z%d" % i) for i in range(PACK)]
+        for c, (a, b) in enumerate(X_CHUNKS):
+            width = b - a
+            x_bf = held.tile([P, width, PACK], BF16, name="x_bf%d" % c, align_bytes=64)
+            src = x_raw[c][:].rearrange("p i c -> p c i")
+            if c == len(X_CHUNKS) - 1:
+                nc.vector.tensor_copy(out=x_bf[:, :X_SPLIT, :], in_=src[:, :X_SPLIT, :])
+                nc.scalar.copy(out=x_bf[:, X_SPLIT:, :], in_=src[:, X_SPLIT:, :])
+            else:
+                nc.vector.tensor_copy(out=x_bf[:], in_=src)
+            x_codes = held.tile([P, width], U32, name="x_codes%d" % c, align_bytes=64)
+            x_scale = held.tile([P, width], U8, name="x_scale%d" % c, align_bytes=64)
+            nc.vector.quantize_mx(out=x_codes[:].bitcast(FP8X4), scales=x_scale[:],
+                                  in_=x_bf[:].rearrange("p c i -> p (c i)"))
+            for i in range(PACK):
+                acc = psum.tile([P, width], F32, name="acc%d_%d" % (c, i))
+                nc.tensor.matmul_mx(out=acc[:],
+                                    lhsT=w_codes[:, 2 * P * i : 2 * P * (i + 1)].bitcast(FP4X4),
+                                    lhsT_scale=w_scale[:, P * i : P * (i + 1)],
+                                    rhs=x_codes[:].bitcast(FP8X4), rhs_scale=x_scale[:],
+                                    start=True, stop=True)
+                nc.scalar.copy(out=z[i][:, a:b], in_=acc[:])
+
+        y_rows = out_0.rearrange("(p i) j -> p i j", i=PACK)
+        y_words = out_1[0].rearrange("p j i -> p (j i)").bitcast(I32)
+        y_scale = held.tile([P, J], U8, name="y_scale", align_bytes=64)
+        for c, (a, b) in enumerate(J_CHUNKS):
+            width = b - a
+            y = held.tile([P, PACK, width], F32, name="y%d" % c)
+            u = []
+            for i in range(PACK):
+                tile = picks.tile([P, width], F32, name="u")
+                nc.vector.tensor_copy(tile[:], z[i][:].indirect(offsets[:, a // 16 : b // 16]))
+                last = min(b, J - 1)
+                nc.scalar.activation(before[i][:, LEAD + a : LEAD + last], tile[:, : last - a], COPY,
+                                     scale=step[:, i : i + 1])
+                u.append(tile)
+            for i in range(PACK):
+                nc.vector.scalar_tensor_tensor(y[:, i, :], u[i][:], own[:, i : i + 1],
+                                               before[i][:, LEAD - 1 + a : LEAD - 1 + b], ALU.mult, ALU.subtract)
+                nc.sync.dma_start(out=y_rows[:, i, a:b], in_=y[:, i, :])
+            y_bf = held.tile([P, width, PACK], BF16, name="y_bf%d" % c, align_bytes=64)
+            src = y[:].rearrange("p i j -> p j i")
+            if c == len(J_CHUNKS) - 1:
+                nc.vector.tensor_copy(out=y_bf[:, :Y_SPLIT, :], in_=src[:, :Y_SPLIT, :])
+                nc.scalar.copy(out=y_bf[:, Y_SPLIT:, :], in_=src[:, Y_SPLIT:, :])
+            else:
+                nc.scalar.copy(out=y_bf[:], in_=src)
+            y_codes = held.tile([P, width], U32, name="y_codes%d" % c, align_bytes=64)
+            nc.vector.quantize_mx(out=y_codes[:].bitcast(FP8X4), scales=y_scale[:, a:b],
+                                  in_=y_bf[:].rearrange("p j i -> p (j i)"))
+            nc.sync.dma_start(out=y_words[:, a:b], in_=y_codes[:].bitcast(I32))
+        for q in range(4):
+            eng = nc.scalar if q % 2 else nc.sync
+            eng.dma_start(out=out_2[0, 4 * q : 4 * q + 4, :].bitcast(I32),
+                          in_=y_scale[32 * q : 32 * q + 4, :].bitcast(I32))

@@ -25,6 +25,11 @@ J_CHUNKS = ((0, 256), (256, 512))
 Y_SPLIT = 168
 
 
+def weave(copy, dst, src, a, b):
+    copy(out=dst[:, a:b, :].rearrange("p (c n) i -> p c i n", n=4),
+         in_=src[:, :, a:b].rearrange("p i (c n) -> p c i n", n=4))
+
+
 def tile_list_head_steps_in_time_pl_kernel(tc, xt, w_words, w_scales, st, offs, out_0, out_1, out_2):
     nc = tc.nc
     with ExitStack() as ctx:
@@ -33,25 +38,23 @@ def tile_list_head_steps_in_time_pl_kernel(tc, xt, w_words, w_scales, st, offs, 
         psum = ctx.enter_context(tc.psum_pool(name="psum", bufs=1))
 
         x_rows = xt.rearrange("(p i) c -> p i c", i=PACK)
-        x_raw = []
-        for c, (a, b) in enumerate(X_CHUNKS):
-            tile = held.tile([P, PACK, b - a], F32, name="x_raw%d" % c)
-            nc.sync.dma_start(out=tile[:], in_=x_rows[:, :, a:b])
-            x_raw.append(tile)
-        offsets = held.tile([P, J // 16], U16, name="offsets")
-        nc.sync.dma_start(offsets[:], offs)
-
+        x_raw = [held.tile([P, PACK, b - a], F32, name="x_raw%d" % c) for c, (a, b) in enumerate(X_CHUNKS)]
         w_raw = held.tile([P, 2 * N], U8, name="w_raw")
-        nc.scalar.dma_start(out=w_raw[:].bitcast(I32), in_=w_words[0].bitcast(I32))
         ws_raw = held.tile([P, N], U8, name="ws_raw")
-        nc.gpsimd.memset(ws_raw[:].bitcast(I32), 0)
+        offsets = held.tile([P, J // 16], U16, name="offsets")
+        nc.scalar.dma_start(out=w_raw[:].bitcast(I32), in_=w_words[0].bitcast(I32))
         for q in range(4):
-            nc.scalar.dma_start(out=ws_raw[32 * q : 32 * q + 4, :].bitcast(I32),
-                                in_=w_scales[0, 4 * q : 4 * q + 4, :].bitcast(I32))
+            rows = w_scales[0, 4 * q : 4 * q + 4, :].bitcast(I32)
+            queue = nc.scalar if q % 2 else nc.sync
+            queue.dma_start(out=ws_raw[32 * q : 32 * q + 32, :].bitcast(I32),
+                            in_=rows.unsqueeze(0).broadcast_to([8, 4, N // 4]))
+        for c, (a, b) in enumerate(X_CHUNKS):
+            nc.sync.dma_start(out=x_raw[c][:], in_=x_rows[:, :, a:b])
+        nc.sync.dma_start(offsets[:], offs)
         step = held.tile([P, PACK], F32, name="step")
-        nc.gpsimd.dma_start(out=step[:], in_=st.rearrange("(p i) o -> p (i o)", i=PACK))
+        nc.scalar.dma_start(out=step[:], in_=st.rearrange("(p i) o -> p (i o)", i=PACK))
         own = held.tile([P, PACK], F32, name="own")
-        nc.gpsimd.tensor_scalar(own[:], step[:], 1.0, 0.5, ALU.mult, ALU.add)
+        nc.scalar.activation(own[:], step[:], COPY, bias=0.5)
 
         w_codes = held.tile([P, 2 * N], U8, name="w_codes", align_bytes=64)
         nc.vector.tensor_copy(out=w_codes[:].bitcast(U16).rearrange("p (i m) -> p i m", i=PACK),
@@ -64,22 +67,22 @@ def tile_list_head_steps_in_time_pl_kernel(tc, xt, w_words, w_scales, st, offs, 
         for i in range(PACK):
             nc.vector.memset(before[i][:, LEAD - 1 : LEAD], 0.0)
 
+        x_quant = []
         z = [held.tile([P, T], F32, name="z%d" % i) for i in range(PACK)]
         for c, (a, b) in enumerate(X_CHUNKS):
             width = b - a
             x_bf = held.tile([P, width, PACK], BF16, name="x_bf%d" % c, align_bytes=64)
-            src = x_raw[c][:].rearrange("p i c -> p c i")
-            if c == len(X_CHUNKS) - 1:
-                nc.vector.tensor_copy(out=x_bf[:, :X_SPLIT, :], in_=src[:, :X_SPLIT, :])
-                nc.scalar.copy(out=x_bf[:, X_SPLIT:, :], in_=src[:, X_SPLIT:, :])
-            else:
-                nc.vector.tensor_copy(out=x_bf[:], in_=src)
+            weave(nc.vector.tensor_copy, x_bf, x_raw[c], 0, X_SPLIT)
+            weave(nc.scalar.copy, x_bf, x_raw[c], X_SPLIT, width)
             x_codes = held.tile([P, width], U32, name="x_codes%d" % c, align_bytes=64)
             x_scale = held.tile([P, width], U8, name="x_scale%d" % c, align_bytes=64)
             nc.vector.quantize_mx(out=x_codes[:].bitcast(FP8X4), scales=x_scale[:],
                                   in_=x_bf[:].rearrange("p c i -> p (c i)"))
-            for i in range(PACK):
-                acc = psum.tile([P, width], F32, name="acc%d_%d" % (c, i))
+            x_quant.append((x_codes, x_scale))
+        for i in range(PACK):
+            for c, (a, b) in enumerate(X_CHUNKS):
+                x_codes, x_scale = x_quant[c]
+                acc = psum.tile([P, b - a], F32, name="acc%d_%d" % (c, i))
                 nc.tensor.matmul_mx(out=acc[:],
                                     lhsT=w_codes[:, 2 * P * i : 2 * P * (i + 1)].bitcast(FP4X4),
                                     lhsT_scale=w_scale[:, P * i : P * (i + 1)],
@@ -106,12 +109,11 @@ def tile_list_head_steps_in_time_pl_kernel(tc, xt, w_words, w_scales, st, offs, 
                                                before[i][:, LEAD - 1 + a : LEAD - 1 + b], ALU.mult, ALU.subtract)
                 nc.sync.dma_start(out=y_rows[:, i, a:b], in_=y[:, i, :])
             y_bf = held.tile([P, width, PACK], BF16, name="y_bf%d" % c, align_bytes=64)
-            src = y[:].rearrange("p i j -> p j i")
             if c == len(J_CHUNKS) - 1:
-                nc.vector.tensor_copy(out=y_bf[:, :Y_SPLIT, :], in_=src[:, :Y_SPLIT, :])
-                nc.scalar.copy(out=y_bf[:, Y_SPLIT:, :], in_=src[:, Y_SPLIT:, :])
+                weave(nc.vector.tensor_copy, y_bf, y, 0, Y_SPLIT)
+                weave(nc.scalar.copy, y_bf, y, Y_SPLIT, width)
             else:
-                nc.scalar.copy(out=y_bf[:], in_=src)
+                weave(nc.scalar.copy, y_bf, y, 0, width)
             y_codes = held.tile([P, width], U32, name="y_codes%d" % c, align_bytes=64)
             nc.vector.quantize_mx(out=y_codes[:].bitcast(FP8X4), scales=y_scale[:, a:b],
                                   in_=y_bf[:].rearrange("p j i -> p (j i)"))

@@ -20,14 +20,19 @@ P = 128
 PACK = 4
 LEAD = 8
 X_CHUNKS = ((0, 256), (256, 512))
-X_SPLIT = 168
+X_SPLIT = 144
 J_CHUNKS = ((0, 256), (256, 512))
-Y_SPLIT = 168
+Y_SPLIT = 96
 
 
 def weave(copy, dst, src, a, b):
     copy(out=dst[:, a:b, :].rearrange("p (c n) i -> p c i n", n=4),
          in_=src[:, :, a:b].rearrange("p i (c n) -> p c i n", n=4))
+
+
+def quantise(nc, codes, scale, woven, a, b):
+    nc.vector.quantize_mx(out=codes[:, a:b].bitcast(FP8X4), scales=scale[:, a:b],
+                          in_=woven[:, a:b, :].rearrange("p c i -> p (c i)"))
 
 
 def tile_list_head_steps_in_time_pl_kernel(tc, xt, w_words, w_scales, st, offs, out_0, out_1, out_2):
@@ -42,17 +47,17 @@ def tile_list_head_steps_in_time_pl_kernel(tc, xt, w_words, w_scales, st, offs, 
         w_raw = held.tile([P, 2 * N], U8, name="w_raw")
         ws_raw = held.tile([P, N], U8, name="ws_raw")
         offsets = held.tile([P, J // 16], U16, name="offsets")
+        step = held.tile([P, PACK], F32, name="step")
+        nc.sync.dma_start(out=x_raw[0][:], in_=x_rows[:, :, X_CHUNKS[0][0] : X_CHUNKS[0][1]])
         nc.scalar.dma_start(out=w_raw[:].bitcast(I32), in_=w_words[0].bitcast(I32))
         for q in range(4):
             rows = w_scales[0, 4 * q : 4 * q + 4, :].bitcast(I32)
             queue = nc.scalar if q % 2 else nc.sync
             queue.dma_start(out=ws_raw[32 * q : 32 * q + 32, :].bitcast(I32),
                             in_=rows.unsqueeze(0).broadcast_to([8, 4, N // 4]))
-        for c, (a, b) in enumerate(X_CHUNKS):
-            nc.sync.dma_start(out=x_raw[c][:], in_=x_rows[:, :, a:b])
-        nc.sync.dma_start(offsets[:], offs)
-        step = held.tile([P, PACK], F32, name="step")
+        nc.sync.dma_start(out=x_raw[1][:], in_=x_rows[:, :, X_CHUNKS[1][0] : X_CHUNKS[1][1]])
         nc.scalar.dma_start(out=step[:], in_=st.rearrange("(p i) o -> p (i o)", i=PACK))
+        nc.sync.dma_start(offsets[:], offs)
         own = held.tile([P, PACK], F32, name="own")
         nc.scalar.activation(own[:], step[:], COPY, bias=0.5)
 
@@ -63,36 +68,47 @@ def tile_list_head_steps_in_time_pl_kernel(tc, xt, w_words, w_scales, st, offs, 
         nc.vector.tensor_copy(out=w_scale[:].rearrange("p (i m) -> p i m", i=PACK),
                               in_=ws_raw[:].rearrange("p (m i) -> p i m", i=PACK))
 
-        before = [held.tile([P, LEAD + J], F32, name="before%d" % i) for i in range(PACK)]
+        before = [held.tile([P, LEAD + J], F32, name="before%d" % i, tag="before%d" % i, align_bytes=64) for i in range(PACK)]
         for i in range(PACK):
             nc.vector.memset(before[i][:, LEAD - 1 : LEAD], 0.0)
 
         x_quant = []
-        z = [held.tile([P, T], F32, name="z%d" % i) for i in range(PACK)]
         for c, (a, b) in enumerate(X_CHUNKS):
             width = b - a
-            x_bf = held.tile([P, width, PACK], BF16, name="x_bf%d" % c, align_bytes=64)
-            weave(nc.vector.tensor_copy, x_bf, x_raw[c], 0, X_SPLIT)
-            weave(nc.scalar.copy, x_bf, x_raw[c], X_SPLIT, width)
+            x_bf = held.tile([P, width, PACK], BF16, name="x_bf%d" % c, tag="x_bf%d" % c, align_bytes=64)
             x_codes = held.tile([P, width], U32, name="x_codes%d" % c, align_bytes=64)
             x_scale = held.tile([P, width], U8, name="x_scale%d" % c, align_bytes=64)
-            nc.vector.quantize_mx(out=x_codes[:].bitcast(FP8X4), scales=x_scale[:],
-                                  in_=x_bf[:].rearrange("p c i -> p (c i)"))
+            if c == 0:
+                weave(nc.vector.tensor_copy, x_bf, x_raw[c], 0, X_SPLIT)
+                weave(nc.scalar.copy, x_bf, x_raw[c], X_SPLIT, width)
+                quantise(nc, x_codes, x_scale, x_bf, 0, width)
+            else:
+                for h in range(0, width, P):
+                    weave(nc.vector.tensor_copy, x_bf, x_raw[c], h, h + P)
+                for h in range(0, width, P):
+                    quantise(nc, x_codes, x_scale, x_bf, h, h + P)
             x_quant.append((x_codes, x_scale))
+        z = [held.tile([P, T], F32, name="z%d" % i, tag="x_bf1" if i == 2 else "z%d" % i, align_bytes=64)
+             for i in range(PACK)]
         for i in range(PACK):
             for c, (a, b) in enumerate(X_CHUNKS):
                 x_codes, x_scale = x_quant[c]
-                acc = psum.tile([P, b - a], F32, name="acc%d_%d" % (c, i))
-                nc.tensor.matmul_mx(out=acc[:],
-                                    lhsT=w_codes[:, 2 * P * i : 2 * P * (i + 1)].bitcast(FP4X4),
-                                    lhsT_scale=w_scale[:, P * i : P * (i + 1)],
-                                    rhs=x_codes[:].bitcast(FP8X4), rhs_scale=x_scale[:],
-                                    start=True, stop=True)
-                nc.scalar.copy(out=z[i][:, a:b], in_=acc[:])
+                piece = P if (i, c) == (0, 1) else b - a
+                for h in range(0, b - a, piece):
+                    bank = (0, 1, 0) if (i, c) == (PACK - 1, 0) else (i, c, h)
+                    acc = psum.tile([P, piece], F32, name="acc", tag="bank%d_%d_%d" % bank)[:]
+                    nc.tensor.matmul_mx(out=acc,
+                                        lhsT=w_codes[:, 2 * P * i : 2 * P * (i + 1)].bitcast(FP4X4),
+                                        lhsT_scale=w_scale[:, P * i : P * (i + 1)],
+                                        rhs=x_codes[:, h : h + piece].bitcast(FP8X4),
+                                        rhs_scale=x_scale[:, h : h + piece], start=True, stop=True)
+                    copy = nc.vector.tensor_copy if (i, c) == (2, 0) else nc.scalar.copy
+                    copy(out=z[i][:, a + h : a + h + piece], in_=acc)
 
         y_rows = out_0.rearrange("(p i) j -> p i j", i=PACK)
         y_words = out_1[0].rearrange("p j i -> p (j i)").bitcast(I32)
         y_scale = held.tile([P, J], U8, name="y_scale", align_bytes=64)
+        woven = []
         for c, (a, b) in enumerate(J_CHUNKS):
             width = b - a
             y = held.tile([P, PACK, width], F32, name="y%d" % c)
@@ -107,16 +123,21 @@ def tile_list_head_steps_in_time_pl_kernel(tc, xt, w_words, w_scales, st, offs, 
             for i in range(PACK):
                 nc.vector.scalar_tensor_tensor(y[:, i, :], u[i][:], own[:, i : i + 1],
                                                before[i][:, LEAD - 1 + a : LEAD - 1 + b], ALU.mult, ALU.subtract)
-                nc.sync.dma_start(out=y_rows[:, i, a:b], in_=y[:, i, :])
+                if i == PACK - 1 or (c > 0 and i == 1):
+                    first = 0 if c == 0 else i - 1
+                    nc.sync.dma_start(out=y_rows[:, first : i + 1, a:b], in_=y[:, first : i + 1, :])
             y_bf = held.tile([P, width, PACK], BF16, name="y_bf%d" % c, align_bytes=64)
             if c == len(J_CHUNKS) - 1:
                 weave(nc.vector.tensor_copy, y_bf, y, 0, Y_SPLIT)
                 weave(nc.scalar.copy, y_bf, y, Y_SPLIT, width)
             else:
                 weave(nc.scalar.copy, y_bf, y, 0, width)
-            y_codes = held.tile([P, width], U32, name="y_codes%d" % c, align_bytes=64)
+            woven.append(y_bf)
+        for c, (a, b) in enumerate(J_CHUNKS):
+            tag = "before2" if c == 0 else "y_codes"
+            y_codes = held.tile([P, b - a], U32, name="y_codes%d" % c, tag=tag, align_bytes=64)
             nc.vector.quantize_mx(out=y_codes[:].bitcast(FP8X4), scales=y_scale[:, a:b],
-                                  in_=y_bf[:].rearrange("p j i -> p (j i)"))
+                                  in_=woven[c][:].rearrange("p j i -> p (j i)"))
             nc.sync.dma_start(out=y_words[:, a:b], in_=y_codes[:].bitcast(I32))
         for q in range(4):
             eng = nc.scalar if q % 2 else nc.sync

from contextlib import ExitStack

import concourse.mybir as mybir

K, T, J, N = 512, 512, 512, 512
FLOPS = 2 * K * N * T

F32 = mybir.dt.float32
BF16 = mybir.dt.bfloat16
I32 = mybir.dt.int32
U32 = mybir.dt.uint32
U16 = mybir.dt.uint16
U8 = mybir.dt.uint8
FP8X4 = mybir.dt.float8_e4m3fn_x4
FP4X4 = mybir.dt.float4_e2m1fn_x4
ALU = mybir.AluOpType
COPY = mybir.ActivationFunctionType.Copy

P = 128
PACK = 4
LEAD = 8
X_CHUNKS = ((0, 256), (256, 512))
X_SPLIT = 144
J_CHUNKS = ((0, 256), (256, 512))
Y_SPLIT = 96


def weave(copy, dst, src, a, b):
    copy(out=dst[:, a:b, :].rearrange("p (c n) i -> p c i n", n=4),
         in_=src[:, :, a:b].rearrange("p i (c n) -> p c i n", n=4))


def quantise(nc, codes, scale, woven, a, b):
    nc.vector.quantize_mx(out=codes[:, a:b].bitcast(FP8X4), scales=scale[:, a:b],
                          in_=woven[:, a:b, :].rearrange("p c i -> p (c i)"))


def tile_list_head_steps_in_time_pl_kernel(tc, xt, w_words, w_scales, st, offs, out_0, out_1, out_2):
    nc = tc.nc
    with ExitStack() as ctx:
        held = ctx.enter_context(tc.tile_pool(name="held", bufs=1))
        picks = ctx.enter_context(tc.tile_pool(name="picks", bufs=5))
        psum = ctx.enter_context(tc.psum_pool(name="psum", bufs=1))

        x_rows = xt.rearrange("(p i) c -> p i c", i=PACK)
        x_raw = [held.tile([P, PACK, b - a], F32, name="x_raw%d" % c) for c, (a, b) in enumerate(X_CHUNKS)]
        w_raw = held.tile([P, 2 * N], U8, name="w_raw")
        ws_raw = held.tile([P, N], U8, name="ws_raw")
        offsets = held.tile([P, J // 16], U16, name="offsets")
        step = held.tile([P, PACK], F32, name="step")
        nc.sync.dma_start(out=x_raw[0][:], in_=x_rows[:, :, X_CHUNKS[0][0] : X_CHUNKS[0][1]])
        nc.scalar.dma_start(out=w_raw[:].bitcast(I32), in_=w_words[0].bitcast(I32))
        for q in range(4):
            rows = w_scales[0, 4 * q : 4 * q + 4, :].bitcast(I32)
            queue = nc.scalar if q % 2 else nc.sync
            queue.dma_start(out=ws_raw[32 * q : 32 * q + 32, :].bitcast(I32),
                            in_=rows.unsqueeze(0).broadcast_to([8, 4, N // 4]))
        nc.sync.dma_start(out=x_raw[1][:], in_=x_rows[:, :, X_CHUNKS[1][0] : X_CHUNKS[1][1]])
        nc.scalar.dma_start(out=step[:], in_=st.rearrange("(p i) o -> p (i o)", i=PACK))
        nc.sync.dma_start(offsets[:], offs)
        own = held.tile([P, PACK], F32, name="own")
        nc.scalar.activation(own[:], step[:], COPY, bias=0.5)

        w_codes = held.tile([P, 2 * N], U8, name="w_codes", align_bytes=64)
        nc.vector.tensor_copy(out=w_codes[:].bitcast(U16).rearrange("p (i m) -> p i m", i=PACK),
                              in_=w_raw[:].bitcast(U16).rearrange("p (m i) -> p i m", i=PACK))
        w_scale = held.tile([P, N], U8, name="w_scale", align_bytes=64)
        nc.vector.tensor_copy(out=w_scale[:].rearrange("p (i m) -> p i m", i=PACK),
                              in_=ws_raw[:].rearrange("p (m i) -> p i m", i=PACK))

        before = [held.tile([P, LEAD + J], F32, name="before%d" % i, tag="before%d" % i, align_bytes=64) for i in range(PACK)]
        for i in range(PACK):
            nc.vector.memset(before[i][:, LEAD - 1 : LEAD], 0.0)

        x_quant = []
        for c, (a, b) in enumerate(X_CHUNKS):
            width = b - a
            x_bf = held.tile([P, width, PACK], BF16, name="x_bf%d" % c, tag="x_bf%d" % c, align_bytes=64)
            x_codes = held.tile([P, width], U32, name="x_codes%d" % c, align_bytes=64)
            x_scale = held.tile([P, width], U8, name="x_scale%d" % c, align_bytes=64)
            if c == 0:
                weave(nc.vector.tensor_copy, x_bf, x_raw[c], 0, X_SPLIT)
                weave(nc.scalar.copy, x_bf, x_raw[c], X_SPLIT, width)
                quantise(nc, x_codes, x_scale, x_bf, 0, width)
            else:
                for h in range(0, width, P):
                    weave(nc.vector.tensor_copy, x_bf, x_raw[c], h, h + P)
                for h in range(0, width, P):
                    quantise(nc, x_codes, x_scale, x_bf, h, h + P)
            x_quant.append((x_codes, x_scale))
        z = [held.tile([P, T], F32, name="z%d" % i, tag="x_bf1" if i == 2 else "z%d" % i, align_bytes=64)
             for i in range(PACK)]
        for i in range(PACK):
            for c, (a, b) in enumerate(X_CHUNKS):
                x_codes, x_scale = x_quant[c]
                piece = P if (i, c) == (0, 1) else b - a
                for h in range(0, b - a, piece):
                    bank = (0, 1, 0) if (i, c) == (PACK - 1, 0) else (i, c, h)
                    acc = psum.tile([P, piece], F32, name="acc", tag="bank%d_%d_%d" % bank)[:]
                    nc.tensor.matmul_mx(out=acc,
                                        lhsT=w_codes[:, 2 * P * i : 2 * P * (i + 1)].bitcast(FP4X4),
                                        lhsT_scale=w_scale[:, P * i : P * (i + 1)],
                                        rhs=x_codes[:, h : h + piece].bitcast(FP8X4),
                                        rhs_scale=x_scale[:, h : h + piece], start=True, stop=True)
                    copy = nc.vector.tensor_copy if (i, c) == (2, 0) else nc.scalar.copy
                    copy(out=z[i][:, a + h : a + h + piece], in_=acc)

        y_rows = out_0.rearrange("(p i) j -> p i j", i=PACK)
        y_words = out_1[0].rearrange("p j i -> p (j i)").bitcast(I32)
        y_scale = held.tile([P, J], U8, name="y_scale", align_bytes=64)
        woven = []
        for c, (a, b) in enumerate(J_CHUNKS):
            width = b - a
            y = held.tile([P, PACK, width], F32, name="y%d" % c)
            u = []
            for i in range(PACK):
                tile = picks.tile([P, width], F32, name="u")
                nc.vector.tensor_copy(tile[:], z[i][:].indirect(offsets[:, a // 16 : b // 16]))
                last = min(b, J - 1)
                nc.scalar.activation(before[i][:, LEAD + a : LEAD + last], tile[:, : last - a], COPY,
                                     scale=step[:, i : i + 1])
                u.append(tile)
            for i in range(PACK):
                nc.vector.scalar_tensor_tensor(y[:, i, :], u[i][:], own[:, i : i + 1],
                                               before[i][:, LEAD - 1 + a : LEAD - 1 + b], ALU.mult, ALU.subtract)
                if i == PACK - 1 or (c > 0 and i == 1):
                    first = 0 if c == 0 else i - 1
                    nc.sync.dma_start(out=y_rows[:, first : i + 1, a:b], in_=y[:, first : i + 1, :])
            y_bf = held.tile([P, width, PACK], BF16, name="y_bf%d" % c, align_bytes=64)
            if c == len(J_CHUNKS) - 1:
                weave(nc.vector.tensor_copy, y_bf, y, 0, Y_SPLIT)
                weave(nc.scalar.copy, y_bf, y, Y_SPLIT, width)
            else:
                weave(nc.scalar.copy, y_bf, y, 0, width)
            woven.append(y_bf)
        for c, (a, b) in enumerate(J_CHUNKS):
            tag = "before2" if c == 0 else "y_codes"
            y_codes = held.tile([P, b - a], U32, name="y_codes%d" % c, tag=tag, align_bytes=64)
            nc.vector.quantize_mx(out=y_codes[:].bitcast(FP8X4), scales=y_scale[:, a:b],
                                  in_=woven[c][:].rearrange("p j i -> p (j i)"))
            nc.sync.dma_start(out=y_words[:, a:b], in_=y_codes[:].bitcast(I32))
        for q in range(4):
            eng = nc.scalar if q % 2 else nc.sync
            eng.dma_start(out=out_2[0, 4 * q : 4 * q + 4, :].bitcast(I32),
                          in_=y_scale[32 * q : 32 * q + 4, :].bitcast(I32))
